import numpy as np
import ml_dtypes


def mxq(x, axis, fmt="e4m3"):
    dtype, down = {"e4m3": (ml_dtypes.float8_e4m3fn, 7), "e5m2": (ml_dtypes.float8_e5m2, 14)}[fmt]
    v = np.moveaxis(np.asarray(x, np.float32).astype(ml_dtypes.bfloat16).astype(np.float64), axis, -1)
    blocks = v.reshape(v.shape[:-1] + (-1, 32))
    amax = np.abs(blocks).max(-1, keepdims=True)
    byte = np.maximum(np.where(amax > 0, np.frexp(amax)[1] - 1 + 127, 0) - down, 1)
    scale = np.exp2(byte - 127.0)
    codes = (blocks / scale).astype(np.float32).astype(dtype).astype(np.float64)
    return np.moveaxis((codes * scale).reshape(v.shape), -1, axis)


WIDE = False


def mx_kscale(k):
    if not WIDE:
        return np.ones(k)
    levels = np.array([30, -30])
    if k % 512:
        return np.exp2(np.random.permutation(np.resize(levels, k // 32))).repeat(32)
    a = np.empty((k // 512, 16))
    for p in range(k // 512):
        a[p, :8] = np.random.permutation(np.resize(levels, 8))
        for g in range(8):
            far = levels[np.abs(levels - a[p, g]) >= 10]
            a[p, g + 8] = far[np.random.randint(len(far))]
    return np.exp2(a.ravel()).repeat(32)


def f64(x):
    return np.asarray(x).astype(np.float64)


def striped(idx):
    return np.tile(np.asarray(idx).reshape(-1, 16).T, (8, 1)).astype(np.uint16)


def unstriped(offs):
    return offs[:16].T.reshape(-1).astype(np.int64)


E2M1 = np.array([0.0, 0.5, 1.0, 1.5, 2.0, 3.0, 4.0, 6.0, -0.0, -0.5, -1.0, -1.5, -2.0, -3.0, -4.0, -6.0])


def pack_weight(w, fmt):
    k, n = w.shape
    w = f64(np.asarray(w, np.float32).astype(ml_dtypes.bfloat16)).reshape(k // 32, 32, n)
    amax = np.abs(w).max(1)
    if fmt in ("e4m3", "e5m2"):
        byte = np.frexp(amax)[1] - 1 + 127 - (7 if fmt == "e4m3" else 14)
    else:
        mant, ex = np.frexp(amax / 6.0)
        byte = np.where(mant > 0.5, ex, ex - 1) + 127
    byte = np.clip(np.where(amax > 0, byte, 1), 1, 254)
    scaled = (w * np.exp2(127.0 - byte)[:, None, :]).reshape(k, n).astype(np.float32)
    by_word = np.ascontiguousarray(scaled.reshape(k // 512, 128, 4, n).transpose(0, 1, 3, 2))
    if fmt in ("e4m3", "e5m2"):
        words = by_word.astype(ml_dtypes.float8_e4m3fn if fmt == "e4m3" else ml_dtypes.float8_e5m2).view(np.uint8)
    else:
        c = by_word.astype(ml_dtypes.float4_e2m1fn).view(np.uint8) & 0xF
        words = (c[..., 0::2] | (c[..., 1::2] << 4)).reshape(k // 512, 128, 2 * n)
    return np.ascontiguousarray(words), np.ascontiguousarray(byte.astype(np.uint8).reshape(k // 512, 16, n))


def unpack_weight(words, scales, fmt):
    g, _, n = scales.shape
    words = np.ascontiguousarray(words).reshape(g, 128, n, -1)
    if fmt in ("e4m3", "e5m2"):
        vals = words.view(ml_dtypes.float8_e4m3fn if fmt == "e4m3" else ml_dtypes.float8_e5m2).astype(np.float64)
    else:
        nib = np.empty((g, 128, n, 4), np.uint8)
        nib[..., 0::2] = words & 0xF
        nib[..., 1::2] = words >> 4
        vals = E2M1[nib]
    vals = vals * np.repeat(np.exp2(scales.astype(np.float64) - 127.0), 8, axis=1)[..., None]
    return vals.transpose(0, 1, 3, 2).reshape(g * 512, n)


def bf(x):
    return np.asarray(x, np.float32).astype(ml_dtypes.bfloat16)


def planes(Y):
    r, m = Y.shape
    b = f64(bf(Y)).reshape(r // 32, 32, m)
    amax = np.abs(b).max(1)
    byte = np.clip(np.where(amax > 0, np.frexp(amax)[1] - 1 + 127 - 7, 1), 1, 254)
    codes = (b * np.exp2(127.0 - byte)[:, None, :]).reshape(r, m).astype(np.float32).astype(ml_dtypes.float8_e4m3fn).view(np.uint8)
    words = codes.reshape(r // 512, 128, 4, m).transpose(0, 1, 3, 2)
    return np.ascontiguousarray(words), np.ascontiguousarray(byte.astype(np.uint8).reshape(r // 512, 16, m))


K, T, J, S, R, F, Z, V, N, Q = 512, 512, 256, 512, 512, 512, 1024, 512, 512, 64


def setup_inputs():
    n = np.random.standard_normal
    idx = np.random.permutation(T)[:J]
    idx2 = np.random.permutation(S)[:J]
    idx3 = np.random.permutation(Z)[:J]
    idx4 = np.random.permutation(V)[:J]
    fk = mx_kscale(K)
    fr = mx_kscale(R)
    ff = mx_kscale(F)
    wp = pack_weight(n((K, R)) * 1 / np.sqrt(K) * fk[:, None] * fr, "e5m2")
    xop = pack_weight(n((F, Z)) / ff[:, None], "e5m2")
    w2p = pack_weight(n((F, R)) * 1 / np.sqrt(F) * ff[:, None] * fr, "e4m3")
    wbp = pack_weight(n((R, N)) * 1 / np.sqrt(R) / fr[:, None], "e2m1")
    return {
        "xa": (n((K, T))).astype(np.float32),
        "xb": (n((K, S))).astype(np.float32),
        "fk": (np.random.uniform(0.5, 2.0, (K, 1)) / fk[:, None]).astype(np.float32),
        "w_words": wp[0],
        "w_scales": wp[1],
        "xo_words": xop[0],
        "xo_scales": xop[1],
        "w2_words": w2p[0],
        "w2_scales": w2p[1],
        "tb": (n((R, V)) * 0.7 * fr[:, None]).astype(np.float32),
        "wb_words": wbp[0],
        "wb_scales": wbp[1],
        "rw": (np.random.uniform(0.5, 2.0, (1, J))).astype(np.float32),
        "qw": (np.random.uniform(0.5, 2.0, (1, Q))).astype(np.float32),
        "offs": striped(idx),
        "offs2": striped(idx2),
        "offs3": striped(idx3),
        "offs4": striped(idx4),
    }


def reference(xa, xb, fk, w_words, w_scales, xo_words, xo_scales, w2_words, w2_scales, tb, wb_words, wb_scales, rw, qw, offs, offs2, offs3, offs4):
    idx = unstriped(offs)
    idx2 = unstriped(offs2)
    idx3 = unstriped(offs3)
    idx4 = unstriped(offs4)
    wu = unpack_weight(w_words, w_scales, "e5m2")
    xou = unpack_weight(xo_words, xo_scales, "e5m2")
    w2u = unpack_weight(w2_words, w2_scales, "e4m3")
    wbu = unpack_weight(wb_words, wb_scales, "e2m1")
    u = f64(xa)[:, idx] * f64(xb)[:, idx2] * f64(fk)
    uq = mxq(u, 0, "e5m2")
    xoidx3g = xou[:, idx3]
    a = wu.T @ uq + w2u.T @ xoidx3g
    hid = np.maximum(a - f64(tb)[:, idx4], 0.0)
    hidq = mxq(hid, 0, "e5m2")
    p = wbu.T @ hidq
    y = (p * f64(rw)).reshape(N, Q, J // Q).sum(axis=2) * f64(qw)
    words, scales = planes(y)
    return y, words, scales

@@ -1,0 +1,208 @@
+from contextlib import ExitStack
+
+import concourse.mybir as mybir
+from concourse.masks import make_identity
+
+F32 = mybir.dt.float32
+BF16 = mybir.dt.bfloat16
+I32 = mybir.dt.int32
+U32 = mybir.dt.uint32
+U16 = mybir.dt.uint16
+U8 = mybir.dt.uint8
+E4M3 = mybir.dt.float8_e4m3fn_x4
+E5M2 = mybir.dt.float8_e5m2_x4
+E2M1 = mybir.dt.float4_e2m1fn_x4
+MULT = mybir.AluOpType.mult
+ADD = mybir.AluOpType.add
+SUB = mybir.AluOpType.subtract
+MAX = mybir.AluOpType.max
+COPY = mybir.ActivationFunctionType.Copy
+
+P = 128
+PACK = 4
+J = 256
+HALF = J // 2
+Q = 64
+C = 512
+Z = 1024
+
+FLOPS = 3 * 2 * 512 * 512 * 256
+
+
+def tile_list_sum_entryproducts_othertable_overtable_groupsums_pl_kernel(tc, xa, xb, fk, w_words, w_scales, xo_words, xo_scales, w2_words, w2_scales, tb, wb_words, wb_scales, rw, qw, offs, offs2, offs3, offs4, out_0, out_1, out_2):
+    nc = tc.nc
+    with ExitStack() as ctx:
+        sb = ctx.enter_context(tc.tile_pool(name="sb", bufs=1))
+        ps = ctx.enter_context(tc.psum_pool(name="ps", bufs=1))
+        ctx.enter_context(nc.allow_non_contiguous_dma(reason="small per-partition factors"))
+
+        def tile(name, shape, dtype):
+            return sb.tile(shape, dtype, name=name, align_bytes=64)
+
+        def load_scales(queue, dst, src):
+            for quad in range(4):
+                queue.dma_start(out=dst[32 * quad : 32 * quad + 4, :].bitcast(I32), in_=src[0, 4 * quad : 4 * quad + 4, :].bitcast(I32))
+
+        def load_words(dst, src):
+            nc.sync.dma_start(out=dst[:].bitcast(I32), in_=src[0].rearrange("p n t -> p (n t)").bitcast(I32))
+
+        def load_rows(name, src, t0, t1):
+            dst = tile(name, [P, t1 - t0, C], F32)
+            nc.sync.dma_start(out=dst[:], in_=src.rearrange("(p t) c -> p t c", t=PACK)[:, t0:t1, :])
+            return [dst[:, t, :] for t in range(t1 - t0)]
+
+        def load_list(name, src):
+            dst = sb.tile([P, J // 16], U16, name=name)
+            nc.sync.dma_start(dst[:], src)
+            return dst
+
+        ws_raw = tile("ws_raw", [P, C], U8)
+        w2s_raw = tile("w2s_raw", [P, C], U8)
+        nc.vector.memset(ws_raw[:].bitcast(I32), 0)
+        nc.vector.memset(w2s_raw[:].bitcast(I32), 0)
+        xos = tile("xos", [P, Z], U8)
+        wbs_raw = tile("wbs_raw", [P, C], U8)
+        nc.gpsimd.memset(xos[:].bitcast(I32), 0)
+        nc.gpsimd.memset(wbs_raw[:].bitcast(I32), 0)
+        cq = tile("cq", [P, PACK], F32)
+        nc.vector.memset(cq[:], 0.0)
+
+        l2 = load_list("l2", offs2)
+        xb_t = load_rows("xb01", xb, 0, 2)
+        l1 = load_list("l1", offs)
+        xa_t = load_rows("xa01", xa, 0, 2)
+        load_scales(nc.scalar, ws_raw, w_scales)
+        load_scales(nc.gpsimd, xos, xo_scales)
+        load_scales(nc.gpsimd, wbs_raw, wb_scales)
+        ident = tile("ident", [P, P], F32)
+        make_identity(nc, ident[:])
+        fk_sb = tile("fk_sb", [P, PACK], F32)
+        nc.sync.dma_start(out=fk_sb[:], in_=fk.rearrange("(p t) o -> p (t o)", t=PACK))
+        xb_t = xb_t + load_rows("xb23", xb, 2, 4)
+        xa_t = xa_t + load_rows("xa23", xa, 2, 4)
+        load_scales(nc.sync, w2s_raw, w2_scales)
+        l3 = load_list("l3", offs3)
+        xow = tile("xow", [P, Z], U32)
+        load_words(xow, xo_words)
+        w2_raw = tile("w2_raw", [P, C], U32)
+        load_words(w2_raw, w2_words)
+        w_raw = tile("w_raw", [P, C], U32)
+        load_words(w_raw, w_words)
+        l4 = load_list("l4", offs4)
+        rw_sb = tile("rw_sb", [Q, PACK], F32)
+        qw_sb = tile("qw_sb", [Q, 1], F32)
+        nc.sync.dma_start(out=rw_sb[:], in_=rw[0].rearrange("(q i) -> q i", i=PACK))
+        nc.sync.dma_start(out=qw_sb[:], in_=qw.rearrange("o q -> q o"))
+        wb_raw = tile("wb_raw", [P, 2 * C], U8)
+        nc.sync.dma_start(out=wb_raw[:].bitcast(I32), in_=wb_words[0].bitcast(I32))
+        tb_t = load_rows("tb01", tb, 0, 2) + load_rows("tb2", tb, 2, 3) + load_rows("tb3", tb, 3, 4)
+
+        def gather(on_scalar, dst, window, offsets):
+            if on_scalar:
+                nc.scalar.activation(dst, window.indirect(offsets), COPY)
+            else:
+                nc.vector.tensor_copy(dst, window.indirect(offsets))
+
+        def deal_scales(name, raw):
+            dst = tile(name, [P, C], U8)
+            nc.vector.tensor_copy(out=dst[:].rearrange("p (t m) -> p m t", t=PACK), in_=raw[:].rearrange("p (m t) -> p m t", t=PACK))
+            return dst
+
+        ga = tile("ga", [P, PACK, J], F32)
+        gb = tile("gb", [P, PACK, J], F32)
+        prod = tile("prod", [P, PACK, J], F32)
+        ws = deal_scales("ws", ws_raw)
+        for t in range(PACK):
+            last = t == PACK - 1
+            gather(last, gb[:, t, :], xb_t[t], l2[:])
+            gather(not last, ga[:, t, :], xa_t[t], l1[:])
+            nc.vector.scalar_tensor_tensor(out=prod[:, t, :], in0=ga[:, t, :], scalar=fk_sb[:, t : t + 1], in1=gb[:, t, :], op0=MULT, op1=MULT)
+        w2s = deal_scales("w2s", w2s_raw)
+
+        u_bf = tile("u_bf", [P, J, PACK], BF16)
+        u_codes = tile("u_codes", [P, J], U32)
+        u_scales = tile("u_scales", [P, J], U8)
+        halves = [slice(0, HALF), slice(HALF, J)]
+        for h in halves:
+            nc.vector.tensor_copy(out=u_bf[:, h, :], in_=prod[:, :, h].rearrange("p t j -> p j t"))
+        for h in halves:
+            nc.vector.quantize_mx(out=u_codes[:, h].bitcast(E5M2), scales=u_scales[:, h], in_=u_bf[:, h, :].rearrange("p j t -> p (j t)"))
+
+        xg_codes = tile("xg_codes", [P, J], U32)
+        xg_scales = tile("xg_scales", [P, J], U8)
+        nc.vector.tensor_copy(xg_codes[:], xow[:].indirect(l3[:]))
+        nc.vector.tensor_copy(xg_scales[:], xos[:].indirect(l3[:]))
+
+        def deal(dst, src):
+            nc.scalar.copy(out=dst.rearrange("p (t m) -> p m t", t=PACK), in_=src.rearrange("p (m t) -> p m t", t=PACK))
+
+        w2_d = tile("w2_d", [P, C], U32)
+        w_d = tile("w_d", [P, C], U32)
+        wb_d = tile("wb_d", [P, 2 * C], U8)
+        deal(w2_d[:], w2_raw[:])
+        deal(w_d[:], w_raw[:])
+        deal(wb_d[:].bitcast(U16), wb_raw[:].bitcast(U16))
+
+        a_ps = [ps.tile([P, J], F32, name="a%d" % t, tag="a%d" % t) for t in range(PACK)]
+        for t in range(PACK):
+            cols = slice(t * P, (t + 1) * P)
+            nc.tensor.matmul_mx(out=a_ps[t][:], lhsT=w2_d[:, cols].bitcast(E4M3), lhsT_scale=w2s[:, cols], rhs=xg_codes[:].bitcast(E5M2), rhs_scale=xg_scales[:], start=True, stop=False)
+        for t in range(PACK):
+            cols = slice(t * P, (t + 1) * P)
+            nc.tensor.matmul_mx(out=a_ps[t][:], lhsT=w_d[:, cols].bitcast(E5M2), lhsT_scale=ws[:, cols], rhs=u_codes[:].bitcast(E5M2), rhs_scale=u_scales[:], start=False, stop=True)
+
+        wbs = deal_scales("wbs", wbs_raw)
+        nc.vector.tensor_scalar(out=cq[0:Q, :], in0=rw_sb[:], scalar1=qw_sb[:], scalar2=None, op0=MULT)
+        c_ps = ps.tile([P, PACK, P], F32, name="c_ps", tag="p3")
+        for i in range(PACK):
+            nc.tensor.transpose(c_ps[:, i, :], cq[:, i : i + 1].to_broadcast([P, P]), ident[:])
+        c_bc = tile("c_bc", [P, Q, PACK], F32)
+
+        gt = tile("gt", [P, PACK, J], F32)
+        diff = tile("diff", [P, PACK, J], F32)
+        for t in range(PACK):
+            if t < PACK - 1:
+                gather(True, gt[:, t, :], tb_t[t], l4[:])
+                nc.vector.tensor_tensor(out=diff[:, t, :], in0=a_ps[t][:], in1=gt[:, t, :], op=SUB)
+            else:
+                for hi, h in enumerate(halves):
+                    gather(hi == 1, gt[:, t, h], tb_t[t], l4[:, 8 * hi : 8 * hi + 8])
+                for h in halves:
+                    nc.vector.tensor_tensor(out=diff[:, t, h], in0=a_ps[t][:, h], in1=gt[:, t, h], op=SUB)
+        nc.scalar.copy(out=c_bc[:], in_=c_ps[:, :, 0:Q].rearrange("p i q -> p q i"))
+
+        h_bf = tile("h_bf", [P, J, PACK], BF16)
+        h_codes = tile("h_codes", [P, J], U32)
+        h_scales = tile("h_scales", [P, J], U8)
+        for h in halves:
+            nc.vector.tensor_scalar(out=h_bf[:, h, :], in0=diff[:, :, h].rearrange("p t j -> p j t"), scalar1=0.0, scalar2=None, op0=MAX)
+        for h in halves:
+            nc.vector.quantize_mx(out=h_codes[:, h].bitcast(E5M2), scales=h_scales[:, h], in_=h_bf[:, h, :].rearrange("p j t -> p (j t)"))
+
+        weighted = tile("weighted", [P, 2, PACK, HALF], F32)
+        c_flat = c_bc[:].rearrange("p q i -> p (q i)")
+        for hi, h in enumerate(halves):
+            for tp in range(2):
+                bank = ps.tile([P, 2, HALF], F32, name="p%d" % (2 * hi + tp), tag="p%d" % (2 * hi + tp))
+                for e in range(2):
+                    t = 2 * tp + e
+                    nc.tensor.matmul_mx(out=bank[:, e, :], lhsT=wb_d[:, 2 * t * P : 2 * (t + 1) * P].bitcast(E2M1), lhsT_scale=wbs[:, t * P : (t + 1) * P], rhs=h_codes[:, h].bitcast(E5M2), rhs_scale=h_scales[:, h], start=True, stop=True)
+                nc.vector.tensor_tensor(out=weighted[:, hi, 2 * tp : 2 * tp + 2, :], in0=bank[:], in1=c_flat[:, h].unsqueeze(1).to_broadcast([P, 2, HALF]), op=MULT)
+
+        pairs = tile("pairs", [P, PACK, Q, 2], F32)
+        for hi in range(2):
+            four = weighted[:, hi, :, :].rearrange("p t (q i) -> p t q i", i=PACK)
+            nc.vector.tensor_tensor(out=pairs[:, :, hi * Q // 2 : (hi + 1) * Q // 2, :], in0=four[:, :, :, 0:2], in1=four[:, :, :, 2:4], op=ADD)
+        y_bf = tile("y_bf", [P, Q, PACK], BF16)
+        y = tile("y", [P, PACK, Q], F32)
+        nc.vector.tensor_tensor(out=y_bf[:], in0=pairs[:, :, :, 0].rearrange("p t q -> p q t"), in1=pairs[:, :, :, 1].rearrange("p t q -> p q t"), op=ADD)
+        nc.vector.tensor_tensor(out=y[:], in0=pairs[:, :, :, 0], in1=pairs[:, :, :, 1], op=ADD)
+        y_codes = tile("y_codes", [P, Q], U32)
+        y_scales = tile("y_scales", [P, Q], U8)
+        nc.vector.quantize_mx(out=y_codes[:].bitcast(E4M3), scales=y_scales[:], in_=y_bf[:].rearrange("p q t -> p (q t)"))
+
+        nc.sync.dma_start(out=out_0.rearrange("(p t) q -> p t q", t=PACK), in_=y[:])
+        nc.scalar.dma_start(out=out_1[0].rearrange("p q t -> p (q t)").bitcast(I32), in_=y_codes[:].bitcast(I32))
+        for quad in range(4):
+            queue = nc.sync if quad % 2 == 0 else nc.scalar
+            queue.dma_start(out=out_2[0, 4 * quad : 4 * quad + 4, :].bitcast(I32), in_=y_scales[32 * quad : 32 * quad + 4, :].bitcast(I32))

@@ -36,11 +36,11 @@ def tile_list_sum_entryproducts_othertable_overtable_groupsums_pl_kernel(tc, xa,
         ps = ctx.enter_context(tc.psum_pool(name="ps", bufs=1))
         ctx.enter_context(nc.allow_non_contiguous_dma(reason="small per-partition factors"))
 
-        def tile(name, shape, dtype):
-            return sb.tile(shape, dtype, name=name, align_bytes=64)
+        def tile(name, shape, dtype, tag=None):
+            return sb.tile(shape, dtype, name=name, tag=tag or name, align_bytes=64)
 
-        def load_scales(queue, dst, src):
-            for quad in range(4):
+        def load_scales(queue, dst, src, quads):
+            for quad in quads:
                 queue.dma_start(out=dst[32 * quad : 32 * quad + 4, :].bitcast(I32), in_=src[0, 4 * quad : 4 * quad + 4, :].bitcast(I32))
 
         def load_words(dst, src):
@@ -58,44 +58,44 @@ def tile_list_sum_entryproducts_othertable_overtable_groupsums_pl_kernel(tc, xa,
 
         ws_raw = tile("ws_raw", [P, C], U8)
         w2s_raw = tile("w2s_raw", [P, C], U8)
-        nc.vector.memset(ws_raw[:].bitcast(I32), 0)
-        nc.vector.memset(w2s_raw[:].bitcast(I32), 0)
         xos = tile("xos", [P, Z], U8)
         wbs_raw = tile("wbs_raw", [P, C], U8)
-        nc.gpsimd.memset(xos[:].bitcast(I32), 0)
-        nc.gpsimd.memset(wbs_raw[:].bitcast(I32), 0)
-        cq = tile("cq", [P, PACK], F32)
-        nc.vector.memset(cq[:], 0.0)
+        nc.vector.memset(xos[:].bitcast(I32), 0)
+        for plane in (ws_raw, w2s_raw, wbs_raw):
+            nc.gpsimd.memset(plane[:].bitcast(I32), 0)
 
+        rw_sb = tile("rw_sb", [Q, PACK], F32)
+        qw_sb = tile("qw_sb", [Q, 1], F32)
+        nc.scalar.dma_start(out=rw_sb[:], in_=rw[0].rearrange("(q i) -> q i", i=PACK))
+        nc.scalar.dma_start(out=qw_sb[:], in_=qw.rearrange("o q -> q o"))
         l2 = load_list("l2", offs2)
         xb_t = load_rows("xb01", xb, 0, 2)
         l1 = load_list("l1", offs)
         xa_t = load_rows("xa01", xa, 0, 2)
-        load_scales(nc.scalar, ws_raw, w_scales)
-        load_scales(nc.gpsimd, xos, xo_scales)
-        load_scales(nc.gpsimd, wbs_raw, wb_scales)
-        ident = tile("ident", [P, P], F32)
-        make_identity(nc, ident[:])
         fk_sb = tile("fk_sb", [P, PACK], F32)
         nc.sync.dma_start(out=fk_sb[:], in_=fk.rearrange("(p t) o -> p (t o)", t=PACK))
         xb_t = xb_t + load_rows("xb23", xb, 2, 4)
         xa_t = xa_t + load_rows("xa23", xa, 2, 4)
-        load_scales(nc.sync, w2s_raw, w2_scales)
-        l3 = load_list("l3", offs3)
+        load_scales(nc.sync, xos, xo_scales, (0, 1))
         xow = tile("xow", [P, Z], U32)
         load_words(xow, xo_words)
-        w2_raw = tile("w2_raw", [P, C], U32)
-        load_words(w2_raw, w2_words)
+        load_scales(nc.sync, xos, xo_scales, (2, 3))
+        l3 = load_list("l3", offs3)
         w_raw = tile("w_raw", [P, C], U32)
         load_words(w_raw, w_words)
+        w2_raw = tile("w2_raw", [P, C], U32)
+        load_words(w2_raw, w2_words)
         l4 = load_list("l4", offs4)
-        rw_sb = tile("rw_sb", [Q, PACK], F32)
-        qw_sb = tile("qw_sb", [Q, 1], F32)
-        nc.sync.dma_start(out=rw_sb[:], in_=rw[0].rearrange("(q i) -> q i", i=PACK))
-        nc.sync.dma_start(out=qw_sb[:], in_=qw.rearrange("o q -> q o"))
+        load_scales(nc.sync, w2s_raw, w2_scales, (0,))
+        tb_t = load_rows("tb01", tb, 0, 2)
+        load_scales(nc.sync, w2s_raw, w2_scales, (1, 2, 3))
+        tb_t = tb_t + load_rows("tb2", tb, 2, 3) + load_rows("tb3", tb, 3, 4)
         wb_raw = tile("wb_raw", [P, 2 * C], U8)
         nc.sync.dma_start(out=wb_raw[:].bitcast(I32), in_=wb_words[0].bitcast(I32))
-        tb_t = load_rows("tb01", tb, 0, 2) + load_rows("tb2", tb, 2, 3) + load_rows("tb3", tb, 3, 4)
+        load_scales(nc.sync, wbs_raw, wb_scales, range(4))
+        load_scales(nc.gpsimd, ws_raw, w_scales, range(4))
+        ident = tile("ident", [P, P], F32)
+        make_identity(nc, ident[:])
 
         def gather(on_scalar, dst, window, offsets):
             if on_scalar:
@@ -103,22 +103,26 @@ def tile_list_sum_entryproducts_othertable_overtable_groupsums_pl_kernel(tc, xa,
             else:
                 nc.vector.tensor_copy(dst, window.indirect(offsets))
 
-        def deal_scales(name, raw):
-            dst = tile(name, [P, C], U8)
+        def deal_scales(name, raw, tag=None):
+            dst = tile(name, [P, C], U8, tag)
             nc.vector.tensor_copy(out=dst[:].rearrange("p (t m) -> p m t", t=PACK), in_=raw[:].rearrange("p (m t) -> p m t", t=PACK))
             return dst
+
+
+        cq = tile("cq", [P, PACK], F32)
+        nc.vector.memset(cq[Q:P, :], 0.0)
+        nc.scalar.activation(cq[0:Q, :], rw_sb[:], COPY, scale=qw_sb[:])
 
         ga = tile("ga", [P, PACK, J], F32)
         gb = tile("gb", [P, PACK, J], F32)
         prod = tile("prod", [P, PACK, J], F32)
-        ws = deal_scales("ws", ws_raw)
-        for t in range(PACK):
-            last = t == PACK - 1
-            gather(last, gb[:, t, :], xb_t[t], l2[:])
-            gather(not last, ga[:, t, :], xa_t[t], l1[:])
-            nc.vector.scalar_tensor_tensor(out=prod[:, t, :], in0=ga[:, t, :], scalar=fk_sb[:, t : t + 1], in1=gb[:, t, :], op0=MULT, op1=MULT)
-        w2s = deal_scales("w2s", w2s_raw)
-
+        for pair in ((0, 1), (2, 3)):
+            for t in pair:
+                gather(t % 2 == 1, gb[:, t, :], xb_t[t], l2[:])
+            for t in pair:
+                gather(t % 2 == 1, ga[:, t, :], xa_t[t], l1[:])
+            for t in pair:
+                nc.vector.scalar_tensor_tensor(out=prod[:, t, :], in0=ga[:, t, :], scalar=fk_sb[:, t : t + 1], in1=gb[:, t, :], op0=MULT, op1=MULT)
         u_bf = tile("u_bf", [P, J, PACK], BF16)
         u_codes = tile("u_codes", [P, J], U32)
         u_scales = tile("u_scales", [P, J], U8)
@@ -128,10 +132,13 @@ def tile_list_sum_entryproducts_othertable_overtable_groupsums_pl_kernel(tc, xa,
         for h in halves:
             nc.vector.quantize_mx(out=u_codes[:, h].bitcast(E5M2), scales=u_scales[:, h], in_=u_bf[:, h, :].rearrange("p j t -> p (j t)"))
 
+        ws = deal_scales("ws", ws_raw, "gb")
         xg_codes = tile("xg_codes", [P, J], U32)
         xg_scales = tile("xg_scales", [P, J], U8)
         nc.vector.tensor_copy(xg_codes[:], xow[:].indirect(l3[:]))
         nc.vector.tensor_copy(xg_scales[:], xos[:].indirect(l3[:]))
+
+        w2s = deal_scales("w2s", w2s_raw)
 
         def deal(dst, src):
             nc.scalar.copy(out=dst.rearrange("p (t m) -> p m t", t=PACK), in_=src.rearrange("p (m t) -> p m t", t=PACK))
@@ -139,24 +146,17 @@ def tile_list_sum_entryproducts_othertable_overtable_groupsums_pl_kernel(tc, xa,
         w2_d = tile("w2_d", [P, C], U32)
         w_d = tile("w_d", [P, C], U32)
         wb_d = tile("wb_d", [P, 2 * C], U8)
-        deal(w2_d[:], w2_raw[:])
         deal(w_d[:], w_raw[:])
-        deal(wb_d[:].bitcast(U16), wb_raw[:].bitcast(U16))
+        deal(w2_d[:], w2_raw[:])
 
         a_ps = [ps.tile([P, J], F32, name="a%d" % t, tag="a%d" % t) for t in range(PACK)]
         for t in range(PACK):
             cols = slice(t * P, (t + 1) * P)
-            nc.tensor.matmul_mx(out=a_ps[t][:], lhsT=w2_d[:, cols].bitcast(E4M3), lhsT_scale=w2s[:, cols], rhs=xg_codes[:].bitcast(E5M2), rhs_scale=xg_scales[:], start=True, stop=False)
+            nc.tensor.matmul_mx(out=a_ps[t][:], lhsT=w_d[:, cols].bitcast(E5M2), lhsT_scale=ws[:, cols], rhs=u_codes[:].bitcast(E5M2), rhs_scale=u_scales[:], start=True, stop=False)
         for t in range(PACK):
             cols = slice(t * P, (t + 1) * P)
-            nc.tensor.matmul_mx(out=a_ps[t][:], lhsT=w_d[:, cols].bitcast(E5M2), lhsT_scale=ws[:, cols], rhs=u_codes[:].bitcast(E5M2), rhs_scale=u_scales[:], start=False, stop=True)
+            nc.tensor.matmul_mx(out=a_ps[t][:], lhsT=w2_d[:, cols].bitcast(E4M3), lhsT_scale=w2s[:, cols], rhs=xg_codes[:].bitcast(E5M2), rhs_scale=xg_scales[:], start=False, stop=True)
 
-        wbs = deal_scales("wbs", wbs_raw)
-        nc.vector.tensor_scalar(out=cq[0:Q, :], in0=rw_sb[:], scalar1=qw_sb[:], scalar2=None, op0=MULT)
-        c_ps = ps.tile([P, PACK, P], F32, name="c_ps", tag="p3")
-        for i in range(PACK):
-            nc.tensor.transpose(c_ps[:, i, :], cq[:, i : i + 1].to_broadcast([P, P]), ident[:])
-        c_bc = tile("c_bc", [P, Q, PACK], F32)
 
         gt = tile("gt", [P, PACK, J], F32)
         diff = tile("diff", [P, PACK, J], F32)
@@ -169,6 +169,13 @@ def tile_list_sum_entryproducts_othertable_overtable_groupsums_pl_kernel(tc, xa,
                     gather(hi == 1, gt[:, t, h], tb_t[t], l4[:, 8 * hi : 8 * hi + 8])
                 for h in halves:
                     nc.vector.tensor_tensor(out=diff[:, t, h], in0=a_ps[t][:, h], in1=gt[:, t, h], op=SUB)
+
+        deal(wb_d[:].bitcast(U16), wb_raw[:].bitcast(U16))
+        wbs = deal_scales("wbs", wbs_raw)
+        c_ps = ps.tile([P, PACK, P], F32, name="c_ps", tag="a0")
+        for i in range(PACK):
+            nc.tensor.transpose(c_ps[:, i, :], cq[:, i : i + 1].to_broadcast([P, P]), ident[:])
+        c_bc = tile("c_bc", [P, Q, PACK], F32)
         nc.scalar.copy(out=c_bc[:], in_=c_ps[:, :, 0:Q].rearrange("p i q -> p q i"))
 
         h_bf = tile("h_bf", [P, J, PACK], BF16)

@@ -61,7 +61,8 @@ def tile_list_sum_entryproducts_othertable_overtable_groupsums_pl_kernel(tc, xa,
         xos = tile("xos", [P, Z], U8)
         wbs_raw = tile("wbs_raw", [P, C], U8)
         nc.vector.memset(xos[:].bitcast(I32), 0)
-        for plane in (ws_raw, w2s_raw, wbs_raw):
+        nc.vector.memset(wbs_raw[:].bitcast(I32), 0)
+        for plane in (ws_raw, w2s_raw):
             nc.gpsimd.memset(plane[:].bitcast(I32), 0)
 
         rw_sb = tile("rw_sb", [Q, PACK], F32)
@@ -69,26 +70,23 @@ def tile_list_sum_entryproducts_othertable_overtable_groupsums_pl_kernel(tc, xa,
         nc.scalar.dma_start(out=rw_sb[:], in_=rw[0].rearrange("(q i) -> q i", i=PACK))
         nc.scalar.dma_start(out=qw_sb[:], in_=qw.rearrange("o q -> q o"))
         l2 = load_list("l2", offs2)
-        xb_t = load_rows("xb01", xb, 0, 2)
+        xb_t = load_rows("xb", xb, 0, 4)
         l1 = load_list("l1", offs)
-        xa_t = load_rows("xa01", xa, 0, 2)
         fk_sb = tile("fk_sb", [P, PACK], F32)
         nc.sync.dma_start(out=fk_sb[:], in_=fk.rearrange("(p t) o -> p (t o)", t=PACK))
-        xb_t = xb_t + load_rows("xb23", xb, 2, 4)
-        xa_t = xa_t + load_rows("xa23", xa, 2, 4)
+        xa_t = load_rows("xa", xa, 0, 4)
+        l3 = load_list("l3", offs3)
         load_scales(nc.sync, xos, xo_scales, (0, 1))
         xow = tile("xow", [P, Z], U32)
         load_words(xow, xo_words)
         load_scales(nc.sync, xos, xo_scales, (2, 3))
-        l3 = load_list("l3", offs3)
         w_raw = tile("w_raw", [P, C], U32)
         load_words(w_raw, w_words)
         w2_raw = tile("w2_raw", [P, C], U32)
         load_words(w2_raw, w2_words)
         l4 = load_list("l4", offs4)
-        load_scales(nc.sync, w2s_raw, w2_scales, (0,))
         tb_t = load_rows("tb01", tb, 0, 2)
-        load_scales(nc.sync, w2s_raw, w2_scales, (1, 2, 3))
+        load_scales(nc.sync, w2s_raw, w2_scales, range(4))
         tb_t = tb_t + load_rows("tb2", tb, 2, 3) + load_rows("tb3", tb, 3, 4)
         wb_raw = tile("wb_raw", [P, 2 * C], U8)
         nc.sync.dma_start(out=wb_raw[:].bitcast(I32), in_=wb_words[0].bitcast(I32))
@@ -105,7 +103,7 @@ def tile_list_sum_entryproducts_othertable_overtable_groupsums_pl_kernel(tc, xa,
 
         def deal_scales(name, raw, tag=None):
             dst = tile(name, [P, C], U8, tag)
-            nc.vector.tensor_copy(out=dst[:].rearrange("p (t m) -> p m t", t=PACK), in_=raw[:].rearrange("p (m t) -> p m t", t=PACK))
+            nc.vector.tensor_copy(out=dst[:].rearrange("p (t m) -> p t m", t=PACK), in_=raw[:].rearrange("p (m t) -> p t m", t=PACK))
             return dst
 
 
@@ -115,24 +113,28 @@ def tile_list_sum_entryproducts_othertable_overtable_groupsums_pl_kernel(tc, xa,
 
         ga = tile("ga", [P, PACK, J], F32)
         gb = tile("gb", [P, PACK, J], F32)
-        prod = tile("prod", [P, PACK, J], F32)
-        for pair in ((0, 1), (2, 3)):
-            for t in pair:
-                gather(t % 2 == 1, gb[:, t, :], xb_t[t], l2[:])
-            for t in pair:
-                gather(t % 2 == 1, ga[:, t, :], xa_t[t], l1[:])
-            for t in pair:
-                nc.vector.scalar_tensor_tensor(out=prod[:, t, :], in0=ga[:, t, :], scalar=fk_sb[:, t : t + 1], in1=gb[:, t, :], op0=MULT, op1=MULT)
+        gbf = tile("gbf", [P, PACK, J], F32)
+        for t in range(PACK):
+            gather(t % 2 == 1, gb[:, t, :], xb_t[t], l2[:])
+        for t in (0, 2, 1, 3):
+            nc.vector.tensor_scalar(out=gbf[:, t, :], in0=gb[:, t, :], scalar1=fk_sb[:, t : t + 1], scalar2=None, op0=MULT)
+        for t in range(PACK):
+            gather(t % 2 == 1, ga[:, t, :], xa_t[t], l1[:])
         u_bf = tile("u_bf", [P, J, PACK], BF16)
         u_codes = tile("u_codes", [P, J], U32)
         u_scales = tile("u_scales", [P, J], U8)
         halves = [slice(0, HALF), slice(HALF, J)]
         for h in halves:
-            nc.vector.tensor_copy(out=u_bf[:, h, :], in_=prod[:, :, h].rearrange("p t j -> p j t"))
+            nc.vector.tensor_tensor(
+                out=u_bf[:, h, :].rearrange("p (c i) t -> p c t i", i=4),
+                in0=ga[:, :, h].rearrange("p t (c i) -> p c t i", i=4),
+                in1=gbf[:, :, h].rearrange("p t (c i) -> p c t i", i=4),
+                op=MULT,
+            )
         for h in halves:
             nc.vector.quantize_mx(out=u_codes[:, h].bitcast(E5M2), scales=u_scales[:, h], in_=u_bf[:, h, :].rearrange("p j t -> p (j t)"))
 
-        ws = deal_scales("ws", ws_raw, "gb")
+        ws = deal_scales("ws", ws_raw, "ga")
         xg_codes = tile("xg_codes", [P, J], U32)
         xg_scales = tile("xg_scales", [P, J], U8)
         nc.vector.tensor_copy(xg_codes[:], xow[:].indirect(l3[:]))
@@ -140,14 +142,14 @@ def tile_list_sum_entryproducts_othertable_overtable_groupsums_pl_kernel(tc, xa,
 
         w2s = deal_scales("w2s", w2s_raw)
 
-        def deal(dst, src):
-            nc.scalar.copy(out=dst.rearrange("p (t m) -> p m t", t=PACK), in_=src.rearrange("p (m t) -> p m t", t=PACK))
+        def deal(dst, src, run):
+            nc.scalar.copy(out=dst.rearrange("p (t b i) -> p b t i", t=PACK, i=run), in_=src.rearrange("p (b i t) -> p b t i", t=PACK, i=run))
 
         w2_d = tile("w2_d", [P, C], U32)
         w_d = tile("w_d", [P, C], U32)
         wb_d = tile("wb_d", [P, 2 * C], U8)
-        deal(w_d[:], w_raw[:])
-        deal(w2_d[:], w2_raw[:])
+        deal(w_d[:], w_raw[:], 4)
+        deal(w2_d[:], w2_raw[:], 4)
 
         a_ps = [ps.tile([P, J], F32, name="a%d" % t, tag="a%d" % t) for t in range(PACK)]
         for t in range(PACK):
@@ -165,12 +167,11 @@ def tile_list_sum_entryproducts_othertable_overtable_groupsums_pl_kernel(tc, xa,
                 gather(True, gt[:, t, :], tb_t[t], l4[:])
                 nc.vector.tensor_tensor(out=diff[:, t, :], in0=a_ps[t][:], in1=gt[:, t, :], op=SUB)
             else:
-                for hi, h in enumerate(halves):
-                    gather(hi == 1, gt[:, t, h], tb_t[t], l4[:, 8 * hi : 8 * hi + 8])
+                gather(True, gt[:, t, :], tb_t[t], l4[:])
                 for h in halves:
                     nc.vector.tensor_tensor(out=diff[:, t, h], in0=a_ps[t][:, h], in1=gt[:, t, h], op=SUB)
 
-        deal(wb_d[:].bitcast(U16), wb_raw[:].bitcast(U16))
+        deal(wb_d[:].bitcast(U16), wb_raw[:].bitcast(U16), 8)
         wbs = deal_scales("wbs", wbs_raw)
         c_ps = ps.tile([P, PACK, P], F32, name="c_ps", tag="a0")
         for i in range(PACK):
@@ -182,7 +183,7 @@ def tile_list_sum_entryproducts_othertable_overtable_groupsums_pl_kernel(tc, xa,
         h_codes = tile("h_codes", [P, J], U32)
         h_scales = tile("h_scales", [P, J], U8)
         for h in halves:
-            nc.vector.tensor_scalar(out=h_bf[:, h, :], in0=diff[:, :, h].rearrange("p t j -> p j t"), scalar1=0.0, scalar2=None, op0=MAX)
+            nc.vector.tensor_scalar(out=h_bf[:, h, :].rearrange("p (c i) t -> p c t i", i=4), in0=diff[:, :, h].rearrange("p t (c i) -> p c t i", i=4), scalar1=0.0, scalar2=None, op0=MAX)
         for h in halves:
             nc.vector.quantize_mx(out=h_codes[:, h].bitcast(E5M2), scales=h_scales[:, h], in_=h_bf[:, h, :].rearrange("p j t -> p (j t)"))
 
@@ -196,14 +197,14 @@ def tile_list_sum_entryproducts_othertable_overtable_groupsums_pl_kernel(tc, xa,
                     nc.tensor.matmul_mx(out=bank[:, e, :], lhsT=wb_d[:, 2 * t * P : 2 * (t + 1) * P].bitcast(E2M1), lhsT_scale=wbs[:, t * P : (t + 1) * P], rhs=h_codes[:, h].bitcast(E5M2), rhs_scale=h_scales[:, h], start=True, stop=True)
                 nc.vector.tensor_tensor(out=weighted[:, hi, 2 * tp : 2 * tp + 2, :], in0=bank[:], in1=c_flat[:, h].unsqueeze(1).to_broadcast([P, 2, HALF]), op=MULT)
 
-        pairs = tile("pairs", [P, PACK, Q, 2], F32)
+        pairs = tile("pairs", [P, Q, PACK, 2], F32)
         for hi in range(2):
-            four = weighted[:, hi, :, :].rearrange("p t (q i) -> p t q i", i=PACK)
-            nc.vector.tensor_tensor(out=pairs[:, :, hi * Q // 2 : (hi + 1) * Q // 2, :], in0=four[:, :, :, 0:2], in1=four[:, :, :, 2:4], op=ADD)
+            four = weighted[:, hi, :, :].rearrange("p t (q i) -> p q t i", i=PACK)
+            nc.vector.tensor_tensor(out=pairs[:, hi * Q // 2 : (hi + 1) * Q // 2, :, :], in0=four[:, :, :, 0:2], in1=four[:, :, :, 2:4], op=ADD)
         y_bf = tile("y_bf", [P, Q, PACK], BF16)
         y = tile("y", [P, PACK, Q], F32)
-        nc.vector.tensor_tensor(out=y_bf[:], in0=pairs[:, :, :, 0].rearrange("p t q -> p q t"), in1=pairs[:, :, :, 1].rearrange("p t q -> p q t"), op=ADD)
-        nc.vector.tensor_tensor(out=y[:], in0=pairs[:, :, :, 0], in1=pairs[:, :, :, 1], op=ADD)
+        nc.vector.tensor_tensor(out=y_bf[:], in0=pairs[:, :, :, 0], in1=pairs[:, :, :, 1], op=ADD)
+        nc.vector.tensor_tensor(out=y[:].rearrange("p t q -> p q t"), in0=pairs[:, :, :, 0], in1=pairs[:, :, :, 1], op=ADD)
         y_codes = tile("y_codes", [P, Q], U32)
         y_scales = tile("y_scales", [P, Q], U8)
         nc.vector.quantize_mx(out=y_codes[:].bitcast(E4M3), scales=y_scales[:], in_=y_bf[:].rearrange("p q t -> p (q t)"))

from contextlib import ExitStack

import concourse.mybir as mybir
from concourse.masks import make_identity

F32 = mybir.dt.float32
BF16 = mybir.dt.bfloat16
I32 = mybir.dt.int32
U32 = mybir.dt.uint32
U16 = mybir.dt.uint16
U8 = mybir.dt.uint8
E4M3 = mybir.dt.float8_e4m3fn_x4
E5M2 = mybir.dt.float8_e5m2_x4
E2M1 = mybir.dt.float4_e2m1fn_x4
MULT = mybir.AluOpType.mult
ADD = mybir.AluOpType.add
SUB = mybir.AluOpType.subtract
MAX = mybir.AluOpType.max
COPY = mybir.ActivationFunctionType.Copy

P = 128
PACK = 4
J = 256
HALF = J // 2
Q = 64
C = 512
Z = 1024

FLOPS = 3 * 2 * 512 * 512 * 256


def tile_list_sum_entryproducts_othertable_overtable_groupsums_pl_kernel(tc, xa, xb, fk, w_words, w_scales, xo_words, xo_scales, w2_words, w2_scales, tb, wb_words, wb_scales, rw, qw, offs, offs2, offs3, offs4, out_0, out_1, out_2):
    nc = tc.nc
    with ExitStack() as ctx:
        sb = ctx.enter_context(tc.tile_pool(name="sb", bufs=1))
        ps = ctx.enter_context(tc.psum_pool(name="ps", bufs=1))
        ctx.enter_context(nc.allow_non_contiguous_dma(reason="small per-partition factors"))

        def tile(name, shape, dtype, tag=None):
            return sb.tile(shape, dtype, name=name, tag=tag or name, align_bytes=64)

        def load_scales(queue, dst, src, quads):
            for quad in quads:
                queue.dma_start(out=dst[32 * quad : 32 * quad + 4, :].bitcast(I32), in_=src[0, 4 * quad : 4 * quad + 4, :].bitcast(I32))

        def load_words(dst, src):
            nc.sync.dma_start(out=dst[:].bitcast(I32), in_=src[0].rearrange("p n t -> p (n t)").bitcast(I32))

        def load_rows(name, src, t0, t1):
            dst = tile(name, [P, t1 - t0, C], F32)
            nc.sync.dma_start(out=dst[:], in_=src.rearrange("(p t) c -> p t c", t=PACK)[:, t0:t1, :])
            return [dst[:, t, :] for t in range(t1 - t0)]

        def load_list(name, src):
            dst = sb.tile([P, J // 16], U16, name=name)
            nc.sync.dma_start(dst[:], src)
            return dst

        ws_raw = tile("ws_raw", [P, C], U8)
        w2s_raw = tile("w2s_raw", [P, C], U8)
        xos = tile("xos", [P, Z], U8)
        wbs_raw = tile("wbs_raw", [P, C], U8)
        nc.vector.memset(xos[:].bitcast(I32), 0)
        nc.vector.memset(wbs_raw[:].bitcast(I32), 0)
        for plane in (ws_raw, w2s_raw):
            nc.gpsimd.memset(plane[:].bitcast(I32), 0)

        rw_sb = tile("rw_sb", [Q, PACK], F32)
        qw_sb = tile("qw_sb", [Q, 1], F32)
        nc.scalar.dma_start(out=rw_sb[:], in_=rw[0].rearrange("(q i) -> q i", i=PACK))
        nc.scalar.dma_start(out=qw_sb[:], in_=qw.rearrange("o q -> q o"))
        l2 = load_list("l2", offs2)
        xb_t = load_rows("xb", xb, 0, 4)
        l1 = load_list("l1", offs)
        fk_sb = tile("fk_sb", [P, PACK], F32)
        nc.sync.dma_start(out=fk_sb[:], in_=fk.rearrange("(p t) o -> p (t o)", t=PACK))
        xa_t = load_rows("xa", xa, 0, 4)
        l3 = load_list("l3", offs3)
        load_scales(nc.sync, xos, xo_scales, (0, 1))
        xow = tile("xow", [P, Z], U32)
        load_words(xow, xo_words)
        load_scales(nc.sync, xos, xo_scales, (2, 3))
        w_raw = tile("w_raw", [P, C], U32)
        load_words(w_raw, w_words)
        w2_raw = tile("w2_raw", [P, C], U32)
        load_words(w2_raw, w2_words)
        l4 = load_list("l4", offs4)
        tb_t = load_rows("tb01", tb, 0, 2)
        load_scales(nc.sync, w2s_raw, w2_scales, range(4))
        tb_t = tb_t + load_rows("tb2", tb, 2, 3) + load_rows("tb3", tb, 3, 4)
        wb_raw = tile("wb_raw", [P, 2 * C], U8)
        nc.sync.dma_start(out=wb_raw[:].bitcast(I32), in_=wb_words[0].bitcast(I32))
        load_scales(nc.sync, wbs_raw, wb_scales, range(4))
        load_scales(nc.gpsimd, ws_raw, w_scales, range(4))
        ident = tile("ident", [P, P], F32)
        make_identity(nc, ident[:])

        def gather(on_scalar, dst, window, offsets):
            if on_scalar:
                nc.scalar.activation(dst, window.indirect(offsets), COPY)
            else:
                nc.vector.tensor_copy(dst, window.indirect(offsets))

        def deal_scales(name, raw, tag=None):
            dst = tile(name, [P, C], U8, tag)
            nc.vector.tensor_copy(out=dst[:].rearrange("p (t m) -> p t m", t=PACK), in_=raw[:].rearrange("p (m t) -> p t m", t=PACK))
            return dst


        cq = tile("cq", [P, PACK], F32)
        nc.vector.memset(cq[Q:P, :], 0.0)
        nc.scalar.activation(cq[0:Q, :], rw_sb[:], COPY, scale=qw_sb[:])

        ga = tile("ga", [P, PACK, J], F32)
        gb = tile("gb", [P, PACK, J], F32)
        gbf = tile("gbf", [P, PACK, J], F32)
        for t in range(PACK):
            gather(t % 2 == 1, gb[:, t, :], xb_t[t], l2[:])
        for t in (0, 2, 1, 3):
            nc.vector.tensor_scalar(out=gbf[:, t, :], in0=gb[:, t, :], scalar1=fk_sb[:, t : t + 1], scalar2=None, op0=MULT)
        for t in range(PACK):
            gather(t % 2 == 1, ga[:, t, :], xa_t[t], l1[:])
        u_bf = tile("u_bf", [P, J, PACK], BF16)
        u_codes = tile("u_codes", [P, J], U32)
        u_scales = tile("u_scales", [P, J], U8)
        halves = [slice(0, HALF), slice(HALF, J)]
        for h in halves:
            nc.vector.tensor_tensor(
                out=u_bf[:, h, :].rearrange("p (c i) t -> p c t i", i=4),
                in0=ga[:, :, h].rearrange("p t (c i) -> p c t i", i=4),
                in1=gbf[:, :, h].rearrange("p t (c i) -> p c t i", i=4),
                op=MULT,
            )
        for h in halves:
            nc.vector.quantize_mx(out=u_codes[:, h].bitcast(E5M2), scales=u_scales[:, h], in_=u_bf[:, h, :].rearrange("p j t -> p (j t)"))

        ws = deal_scales("ws", ws_raw, "ga")
        xg_codes = tile("xg_codes", [P, J], U32)
        xg_scales = tile("xg_scales", [P, J], U8)
        nc.vector.tensor_copy(xg_codes[:], xow[:].indirect(l3[:]))
        nc.vector.tensor_copy(xg_scales[:], xos[:].indirect(l3[:]))

        w2s = deal_scales("w2s", w2s_raw)

        def deal(dst, src, run):
            nc.scalar.copy(out=dst.rearrange("p (t b i) -> p b t i", t=PACK, i=run), in_=src.rearrange("p (b i t) -> p b t i", t=PACK, i=run))

        w2_d = tile("w2_d", [P, C], U32)
        w_d = tile("w_d", [P, C], U32)
        wb_d = tile("wb_d", [P, 2 * C], U8)
        deal(w_d[:], w_raw[:], 4)
        deal(w2_d[:], w2_raw[:], 4)

        a_ps = [ps.tile([P, J], F32, name="a%d" % t, tag="a%d" % t) for t in range(PACK)]
        for t in range(PACK):
            cols = slice(t * P, (t + 1) * P)
            nc.tensor.matmul_mx(out=a_ps[t][:], lhsT=w_d[:, cols].bitcast(E5M2), lhsT_scale=ws[:, cols], rhs=u_codes[:].bitcast(E5M2), rhs_scale=u_scales[:], start=True, stop=False)
        for t in range(PACK):
            cols = slice(t * P, (t + 1) * P)
            nc.tensor.matmul_mx(out=a_ps[t][:], lhsT=w2_d[:, cols].bitcast(E4M3), lhsT_scale=w2s[:, cols], rhs=xg_codes[:].bitcast(E5M2), rhs_scale=xg_scales[:], start=False, stop=True)


        gt = tile("gt", [P, PACK, J], F32)
        diff = tile("diff", [P, PACK, J], F32)
        for t in range(PACK):
            if t < PACK - 1:
                gather(True, gt[:, t, :], tb_t[t], l4[:])
                nc.vector.tensor_tensor(out=diff[:, t, :], in0=a_ps[t][:], in1=gt[:, t, :], op=SUB)
            else:
                gather(True, gt[:, t, :], tb_t[t], l4[:])
                for h in halves:
                    nc.vector.tensor_tensor(out=diff[:, t, h], in0=a_ps[t][:, h], in1=gt[:, t, h], op=SUB)

        deal(wb_d[:].bitcast(U16), wb_raw[:].bitcast(U16), 8)
        wbs = deal_scales("wbs", wbs_raw)
        c_ps = ps.tile([P, PACK, P], F32, name="c_ps", tag="a0")
        for i in range(PACK):
            nc.tensor.transpose(c_ps[:, i, :], cq[:, i : i + 1].to_broadcast([P, P]), ident[:])
        c_bc = tile("c_bc", [P, Q, PACK], F32)
        nc.scalar.copy(out=c_bc[:], in_=c_ps[:, :, 0:Q].rearrange("p i q -> p q i"))

        h_bf = tile("h_bf", [P, J, PACK], BF16)
        h_codes = tile("h_codes", [P, J], U32)
        h_scales = tile("h_scales", [P, J], U8)
        for h in halves:
            nc.vector.tensor_scalar(out=h_bf[:, h, :].rearrange("p (c i) t -> p c t i", i=4), in0=diff[:, :, h].rearrange("p t (c i) -> p c t i", i=4), scalar1=0.0, scalar2=None, op0=MAX)
        for h in halves:
            nc.vector.quantize_mx(out=h_codes[:, h].bitcast(E5M2), scales=h_scales[:, h], in_=h_bf[:, h, :].rearrange("p j t -> p (j t)"))

        weighted = tile("weighted", [P, 2, PACK, HALF], F32)
        c_flat = c_bc[:].rearrange("p q i -> p (q i)")
        for hi, h in enumerate(halves):
            for tp in range(2):
                bank = ps.tile([P, 2, HALF], F32, name="p%d" % (2 * hi + tp), tag="p%d" % (2 * hi + tp))
                for e in range(2):
                    t = 2 * tp + e
                    nc.tensor.matmul_mx(out=bank[:, e, :], lhsT=wb_d[:, 2 * t * P : 2 * (t + 1) * P].bitcast(E2M1), lhsT_scale=wbs[:, t * P : (t + 1) * P], rhs=h_codes[:, h].bitcast(E5M2), rhs_scale=h_scales[:, h], start=True, stop=True)
                nc.vector.tensor_tensor(out=weighted[:, hi, 2 * tp : 2 * tp + 2, :], in0=bank[:], in1=c_flat[:, h].unsqueeze(1).to_broadcast([P, 2, HALF]), op=MULT)

        pairs = tile("pairs", [P, Q, PACK, 2], F32)
        for hi in range(2):
            four = weighted[:, hi, :, :].rearrange("p t (q i) -> p q t i", i=PACK)
            nc.vector.tensor_tensor(out=pairs[:, hi * Q // 2 : (hi + 1) * Q // 2, :, :], in0=four[:, :, :, 0:2], in1=four[:, :, :, 2:4], op=ADD)
        y_bf = tile("y_bf", [P, Q, PACK], BF16)
        y = tile("y", [P, PACK, Q], F32)
        nc.vector.tensor_tensor(out=y_bf[:], in0=pairs[:, :, :, 0], in1=pairs[:, :, :, 1], op=ADD)
        nc.vector.tensor_tensor(out=y[:].rearrange("p t q -> p q t"), in0=pairs[:, :, :, 0], in1=pairs[:, :, :, 1], op=ADD)
        y_codes = tile("y_codes", [P, Q], U32)
        y_scales = tile("y_scales", [P, Q], U8)
        nc.vector.quantize_mx(out=y_codes[:].bitcast(E4M3), scales=y_scales[:], in_=y_bf[:].rearrange("p q t -> p (q t)"))

        nc.sync.dma_start(out=out_0.rearrange("(p t) q -> p t q", t=PACK), in_=y[:])
        nc.scalar.dma_start(out=out_1[0].rearrange("p q t -> p (q t)").bitcast(I32), in_=y_codes[:].bitcast(I32))
        for quad in range(4):
            queue = nc.sync if quad % 2 == 0 else nc.scalar
            queue.dma_start(out=out_2[0, 4 * quad : 4 * quad + 4, :].bitcast(I32), in_=y_scales[32 * quad : 32 * quad + 4, :].bitcast(I32))
